import numpy as np
import ml_dtypes


def mxq(x, axis, fmt="e4m3"):
    dtype, down = {"e4m3": (ml_dtypes.float8_e4m3fn, 7), "e5m2": (ml_dtypes.float8_e5m2, 14)}[fmt]
    v = np.moveaxis(np.asarray(x, np.float32).astype(ml_dtypes.bfloat16).astype(np.float64), axis, -1)
    blocks = v.reshape(v.shape[:-1] + (-1, 32))
    amax = np.abs(blocks).max(-1, keepdims=True)
    byte = np.maximum(np.where(amax > 0, np.frexp(amax)[1] - 1 + 127, 0) - down, 1)
    scale = np.exp2(byte - 127.0)
    codes = (blocks / scale).astype(np.float32).astype(dtype).astype(np.float64)
    return np.moveaxis((codes * scale).reshape(v.shape), -1, axis)


WIDE = False


def mx_kscale(k):
    if not WIDE:
        return np.ones(k)
    levels = np.array([10, -10, 5, -5, 0])
    if k % 512:
        return np.exp2(np.random.permutation(np.resize(levels, k // 32))).repeat(32)
    a = np.empty((k // 512, 16))
    for p in range(k // 512):
        a[p, :8] = np.random.permutation(np.resize(levels, 8))
        for g in range(8):
            far = levels[np.abs(levels - a[p, g]) >= 10]
            a[p, g + 8] = far[np.random.randint(len(far))]
    return np.exp2(a.ravel()).repeat(32)


def f64(x):
    return np.asarray(x).astype(np.float64)


def striped(idx):
    return np.tile(idx.reshape(-1, 16).T, (8, 1)).astype(np.uint16)


def unstriped(offs):
    return offs[:16].T.reshape(-1).astype(np.int64)


E2M1 = np.array([0.0, 0.5, 1.0, 1.5, 2.0, 3.0, 4.0, 6.0, -0.0, -0.5, -1.0, -1.5, -2.0, -3.0, -4.0, -6.0])


def pack_weight(w, fmt):
    k, n = w.shape
    w = f64(np.asarray(w, np.float32).astype(ml_dtypes.bfloat16)).reshape(k // 32, 32, n)
    amax = np.abs(w).max(1)
    if fmt == "e4m3":
        byte = np.frexp(amax)[1] - 1 + 127 - 7
    else:
        mant, ex = np.frexp(amax / 6.0)
        byte = np.where(mant > 0.5, ex, ex - 1) + 127
    byte = np.clip(np.where(amax > 0, byte, 1), 1, 254)
    scaled = (w * np.exp2(127.0 - byte)[:, None, :]).reshape(k, n).astype(np.float32)
    by_word = np.ascontiguousarray(scaled.reshape(k // 512, 128, 4, n).transpose(0, 1, 3, 2))
    if fmt == "e4m3":
        words = by_word.astype(ml_dtypes.float8_e4m3fn).view(np.uint8)
    else:
        c = by_word.astype(ml_dtypes.float4_e2m1fn).view(np.uint8) & 0xF
        words = (c[..., 0::2] | (c[..., 1::2] << 4)).reshape(k // 512, 128, 2 * n)
    return np.ascontiguousarray(words), np.ascontiguousarray(byte.astype(np.uint8).reshape(k // 512, 16, n))


def unpack_weight(words, scales, fmt):
    g, _, n = scales.shape
    words = np.ascontiguousarray(words).reshape(g, 128, n, -1)
    if fmt == "e4m3":
        vals = words.view(ml_dtypes.float8_e4m3fn).astype(np.float64)
    else:
        nib = np.empty((g, 128, n, 4), np.uint8)
        nib[..., 0::2] = words & 0xF
        nib[..., 1::2] = words >> 4
        vals = E2M1[nib]
    vals = vals * np.repeat(np.exp2(scales.astype(np.float64) - 127.0), 8, axis=1)[..., None]
    return vals.transpose(0, 1, 3, 2).reshape(g * 512, n)


def gelu(v):
    return 0.5 * v * (1.0 + np.tanh(np.sqrt(2.0 / np.pi) * (v + 0.044715 * v**3)))


K, M, T, S = 1024, 1024, 4096, 1536


def setup_inputs():
    n = np.random.standard_normal
    s = mx_kscale(K)[:, None]
    u = mx_kscale(512)[:, None]
    v = pack_weight(n((K, T)) * s, "e4m3")
    p_w4 = pack_weight(n((K, M)) / np.sqrt(K) / s, "e2m1")
    return {
        "tab_words": v[0],
        "tab_scales": v[1],
        "w4_words": p_w4[0],
        "w4_scales": p_w4[1],
        "down": (n((K, 512)) / np.sqrt(K) / s * u.T).astype(np.float32),
        "up": (0.5 * n((512, M)) / np.sqrt(512) / u).astype(np.float32),
        "gT": n((M, T)).astype(np.float32),
        "b": (0.3 * n(1024)).astype(np.float32),
        "offs": striped(np.random.permutation(T)[:S]),
    }


def reference(tab_words, tab_scales, w4_words, w4_scales, down, up, gT, b, offs):
    tab_ = unpack_weight(tab_words, tab_scales, "e4m3")[:, unstriped(offs)]
    w4_ = unpack_weight(w4_words, w4_scales, "e2m1")
    down_ = mxq(f64(down), 0, "e4m3")
    up_ = mxq(f64(up), 0, "e4m3")
    h_ = mxq(down_.T @ tab_, 0, "e4m3")
    y = w4_.T @ tab_ + up_.T @ h_
    return (gelu(y + f64(b)[:, None])) * f64(gT)[:, unstriped(offs)]

@@ -1,0 +1,203 @@
+from contextlib import ExitStack
+
+import concourse.mybir as mybir
+from concourse.masks import make_identity
+
+K, M, T, S, R = 1024, 1024, 4096, 1536, 512
+FLOPS = 2 * S * (K * R + K * M + R * M)
+
+F32 = mybir.dt.float32
+BF16 = mybir.dt.bfloat16
+I32 = mybir.dt.int32
+U32 = mybir.dt.uint32
+U16 = mybir.dt.uint16
+U8 = mybir.dt.uint8
+FP8X4 = mybir.dt.float8_e4m3fn_x4
+FP4X4 = mybir.dt.float4_e2m1fn_x4
+
+P = 128
+PACK = 4
+PASSES = K // (P * PACK)
+CHUNK = 512
+CHUNKS = S // CHUNK
+LIST_COLS = CHUNK // 16
+ROW_TILES = M // P
+QUADS = 4
+ALIGN = 64
+
+
+def tile_list_tabgate_gelu_kernel(
+    tc, tab_words, tab_scales, w4_words, w4_scales, down, up, gT, b, offs, out
+):
+    nc = tc.nc
+    mult = mybir.AluOpType.mult
+    gelu = mybir.ActivationFunctionType.Gelu_apprx_tanh
+
+    with ExitStack() as ctx:
+        keep = ctx.enter_context(tc.tile_pool(name="keep", bufs=1))
+        big = ctx.enter_context(tc.tile_pool(name="big", bufs=1))
+        acts = ctx.enter_context(tc.tile_pool(name="acts", bufs=6))
+        psum_h = ctx.enter_context(tc.psum_pool(name="psum_h", bufs=3))
+        psum_y = ctx.enter_context(tc.psum_pool(name="psum_y", bufs=4))
+        psum_b = ctx.enter_context(tc.psum_pool(name="psum_b", bufs=1))
+
+        def big_tile(slot, shape, dtype, name):
+            return big.tile(shape, dtype, name=name, tag="slot%d" % slot, align_bytes=ALIGN)
+
+        def kept(shape, dtype, name):
+            return keep.tile(shape, dtype, name=name, align_bytes=ALIGN)
+
+        down_raw = big_tile(0, [P, PASSES, PACK * R], F32, "down_raw")
+        nc.sync.dma_start(down_raw[:], down.rearrange("(a p j) r -> p a (j r)", a=PASSES, j=PACK))
+        offsets = keep.tile([P, S // 16], U16, name="offsets")
+        nc.sync.dma_start(offsets[:], offs)
+        table = []
+        for a in range(PASSES):
+            words = big_tile(1 + a, [P, T], I32, "table%d" % a)
+            nc.sync.dma_start(words[:], tab_words[a].rearrange("p t i -> p (t i)").bitcast(I32))
+            table.append(words)
+        up_raw = big_tile(3, [P, PACK * M], F32, "up_raw")
+        nc.sync.dma_start(up_raw[:], up.rearrange("(p j) n -> p (j n)", j=PACK))
+        w4 = kept([P, PASSES, 2 * M], U8, "w4")
+        nc.sync.dma_start(w4[:].bitcast(I32), w4_words.rearrange("a p n -> p a n").bitcast(I32))
+
+        gates = []
+
+        def load_gates(i):
+            g = big_tile((4 + i) % 8, [P, T], F32, "gates%d" % i)
+            nc.sync.dma_start(g[:], gT[i * P : (i + 1) * P, :])
+            gates.append(g)
+
+        for i in range(4):
+            load_gates(i)
+
+        scale_rows = kept([P, T], U8, "scale_rows")
+        nc.vector.memset(scale_rows[:].bitcast(I32), 0)
+        nc.scalar.dma_start(
+            scale_rows[0 : 16 * PASSES, :].bitcast(I32), tab_scales.rearrange("a q t -> (a q) t").bitcast(I32)
+        )
+        w4_planes = kept([P, PASSES, M], U8, "w4_planes")
+        nc.vector.memset(w4_planes[:].bitcast(I32), 0)
+        v_planes = kept([P, PASSES * S], U8, "v_planes")
+        nc.vector.memset(v_planes[:].bitcast(I32), 0)
+        b_rows = kept([P, P], F32, "b_rows")
+        nc.vector.memset(b_rows[:], 0.0)
+        for q in range(QUADS):
+            nc.gpsimd.dma_start(
+                w4_planes[32 * q : 32 * q + 4, :, :].bitcast(I32),
+                w4_scales[:, 4 * q : 4 * q + 4, :].rearrange("a r n -> r a n").bitcast(I32),
+            )
+        nc.gpsimd.dma_start(b_rows[0:ROW_TILES, :], b.rearrange("(i p) -> i p", p=P))
+        identity = kept([P, P], F32, "identity")
+        make_identity(nc, identity[:])
+        b_bank = psum_b.tile([P, P], F32, name="b_bank")
+        nc.tensor.transpose(b_bank[:], b_rows[:], identity[:])
+        bias = kept([P, ROW_TILES], F32, "bias")
+        nc.scalar.copy(bias[:], b_bank[:, 0:ROW_TILES])
+
+        picked_scales = kept([P, S], U8, "picked_scales")
+        nc.vector.tensor_copy(picked_scales[:], scale_rows[:].indirect(offsets[:]))
+        for a in range(PASSES):
+            for q in range(QUADS):
+                row = 16 * a + 4 * q
+                nc.gpsimd.dma_start(
+                    v_planes[32 * q : 32 * q + 4, a * S : (a + 1) * S].bitcast(I32),
+                    picked_scales[row : row + 4, :].bitcast(I32),
+                )
+
+        down_codes, down_planes = [], []
+        for a in range(PASSES):
+            grouped = kept([P, PACK * R], BF16, "down_grouped%d" % a)
+            nc.scalar.copy(
+                grouped[:].rearrange("p (t m j) -> p m j t", t=PACK, j=PACK),
+                down_raw[:, a, :].rearrange("p (j m t) -> p m j t", t=PACK, j=PACK),
+            )
+            codes = kept([P, R], U32, "down_codes%d" % a)
+            plane = kept([P, R], U8, "down_plane%d" % a)
+            nc.vector.quantize_mx(out=codes[:].bitcast(FP8X4), scales=plane[:], in_=grouped[:])
+            down_codes.append(codes)
+            down_planes.append(plane)
+        load_gates(4)
+
+        def list_slice(c):
+            return offsets[:, c * LIST_COLS : (c + 1) * LIST_COLS]
+
+        picked = {}
+        for a in range(PASSES):
+            for c in range(CHUNKS):
+                picked[a, c] = kept([P, CHUNK], U32, "picked%d_%d" % (a, c))
+                nc.vector.tensor_copy(picked[a, c][:], table[a][:].bitcast(U32).indirect(list_slice(c)))
+            load_gates(5 + a)
+
+        up_grouped = kept([P, PACK * M], BF16, "up_grouped")
+        nc.vector.tensor_copy(
+            up_grouped[:].rearrange("p (c i j) -> p c j i", i=4, j=PACK),
+            up_raw[:].rearrange("p (j c i) -> p c j i", i=4, j=PACK),
+        )
+        load_gates(7)
+        up_codes = kept([P, M], U32, "up_codes")
+        up_plane = kept([P, M], U8, "up_plane")
+        nc.vector.quantize_mx(out=up_codes[:].bitcast(FP8X4), scales=up_plane[:], in_=up_grouped[:])
+
+        h_codes, h_planes = [], []
+        for c in range(CHUNKS):
+            grouped = kept([P, PACK * CHUNK], BF16, "h_grouped%d" % c)
+            for s in range(CHUNK // P):
+                bank = psum_h.tile([P, PACK, P], F32, name="h_bank")
+                cols = slice(s * P, (s + 1) * P)
+                for t in range(PACK):
+                    for a in range(PASSES):
+                        first = a * S + c * CHUNK + s * P
+                        nc.tensor.matmul_mx(
+                            out=bank[:, t, :],
+                            lhsT=down_codes[a][:, t * P : (t + 1) * P].bitcast(FP8X4),
+                            lhsT_scale=down_planes[a][:, t * P : (t + 1) * P],
+                            rhs=picked[a, c][:, cols].bitcast(FP8X4),
+                            rhs_scale=v_planes[:, first : first + P],
+                            start=(a == 0),
+                            stop=(a == PASSES - 1),
+                        )
+                nc.scalar.copy(
+                    grouped[:, s * PACK * P : (s + 1) * PACK * P].rearrange("p (j t) -> p j t", t=PACK),
+                    bank[:].rearrange("p t j -> p j t"),
+                )
+            codes = kept([P, CHUNK], U32, "h_codes%d" % c)
+            plane = kept([P, CHUNK], U8, "h_plane%d" % c)
+            nc.vector.quantize_mx(out=codes[:].bitcast(FP8X4), scales=plane[:], in_=grouped[:])
+            h_codes.append(codes)
+            h_planes.append(plane)
+
+        for i in range(ROW_TILES):
+            rows = slice(i * P, (i + 1) * P)
+            if i < 2:
+                result = kept([P, S], F32, "result%d" % i)
+            else:
+                result = big_tile((4 + i - 2) % 8, [P, S], F32, "result%d" % i)
+            for c in range(CHUNKS):
+                bank = psum_y.tile([P, CHUNK], F32, name="y_bank")
+                for a in range(PASSES):
+                    first = a * S + c * CHUNK
+                    nc.tensor.matmul_mx(
+                        out=bank[:],
+                        lhsT=w4[:, a, 2 * i * P : 2 * (i + 1) * P].bitcast(FP4X4),
+                        lhsT_scale=w4_planes[:, a, rows],
+                        rhs=picked[a, c][:].bitcast(FP8X4),
+                        rhs_scale=v_planes[:, first : first + CHUNK],
+                        start=(a == 0),
+                        stop=False,
+                    )
+                nc.tensor.matmul_mx(
+                    out=bank[:],
+                    lhsT=up_codes[:, rows].bitcast(FP8X4),
+                    lhsT_scale=up_plane[:, rows],
+                    rhs=h_codes[c][:].bitcast(FP8X4),
+                    rhs_scale=h_planes[c][:],
+                    start=False,
+                    stop=True,
+                )
+                act = acts.tile([P, CHUNK], F32, name="act")
+                nc.scalar.activation(act[:], bank[:], gelu, bias=bias[:, i : i + 1])
+                nc.vector.tensor_tensor(
+                    result[:, c * CHUNK : (c + 1) * CHUNK], gates[i][:].indirect(list_slice(c)), act[:], mult
+                )
+            nc.sync.dma_start(out[rows, :], result[:])

@@ -24,6 +24,8 @@ LIST_COLS = CHUNK // 16
 ROW_TILES = M // P
 QUADS = 4
 ALIGN = 64
+SLOTS = 6
+HALF = M // 2
 
 
 def tile_list_tabgate_gelu_kernel(
@@ -44,52 +46,58 @@ def tile_list_tabgate_gelu_kernel(
         def big_tile(slot, shape, dtype, name):
             return big.tile(shape, dtype, name=name, tag="slot%d" % slot, align_bytes=ALIGN)
 
-        def kept(shape, dtype, name):
-            return keep.tile(shape, dtype, name=name, align_bytes=ALIGN)
+        def kept(shape, dtype, name, tag=None):
+            return keep.tile(shape, dtype, name=name, tag=tag or name, align_bytes=ALIGN)
 
-        down_raw = big_tile(0, [P, PASSES, PACK * R], F32, "down_raw")
-        nc.sync.dma_start(down_raw[:], down.rearrange("(a p j) r -> p a (j r)", a=PASSES, j=PACK))
         offsets = keep.tile([P, S // 16], U16, name="offsets")
         nc.sync.dma_start(offsets[:], offs)
+        down_raw = big_tile(1, [P, PASSES, PACK * R], F32, "down_raw")
+        nc.sync.dma_start(down_raw[:], down.rearrange("(a p j) r -> p a (j r)", a=PASSES, j=PACK))
         table = []
         for a in range(PASSES):
-            words = big_tile(1 + a, [P, T], I32, "table%d" % a)
+            words = big_tile(2 + a, [P, T], I32, "table%d" % a)
             nc.sync.dma_start(words[:], tab_words[a].rearrange("p t i -> p (t i)").bitcast(I32))
             table.append(words)
-        up_raw = big_tile(3, [P, PACK * M], F32, "up_raw")
-        nc.sync.dma_start(up_raw[:], up.rearrange("(p j) n -> p (j n)", j=PACK))
+
+        def load_up(half, raw):
+            nc.sync.dma_start(
+                raw[:].rearrange("p (j n) -> p j n", j=PACK),
+                up[:, half * HALF : (half + 1) * HALF].rearrange("(p j) n -> p j n", j=PACK),
+            )
+            return raw
+
+        up_raw = [load_up(0, big_tile(4, [P, PACK * HALF], F32, "up_raw0"))]
         w4 = kept([P, PASSES, 2 * M], U8, "w4")
         nc.sync.dma_start(w4[:].bitcast(I32), w4_words.rearrange("a p n -> p a n").bitcast(I32))
 
         gates = []
 
         def load_gates(i):
-            g = big_tile((4 + i) % 8, [P, T], F32, "gates%d" % i)
+            g = big_tile(i % SLOTS, [P, T], F32, "gates%d" % i)
             nc.sync.dma_start(g[:], gT[i * P : (i + 1) * P, :])
             gates.append(g)
 
-        for i in range(4):
-            load_gates(i)
+        load_gates(0)
 
         scale_rows = kept([P, T], U8, "scale_rows")
         nc.vector.memset(scale_rows[:].bitcast(I32), 0)
         nc.scalar.dma_start(
-            scale_rows[0 : 16 * PASSES, :].bitcast(I32), tab_scales.rearrange("a q t -> (a q) t").bitcast(I32)
+            scale_rows[0:P:4, :].bitcast(I32), tab_scales.rearrange("a q t -> (a q) t").bitcast(I32)
         )
+        b_rows = kept([P, P], F32, "b_rows")
+        nc.gpsimd.memset(b_rows[:], 0.0)
+        nc.gpsimd.dma_start(b_rows[0:ROW_TILES, :], b.rearrange("(i p) -> i p", p=P))
+        identity = kept([P, P], F32, "identity")
+        make_identity(nc, identity[:])
         w4_planes = kept([P, PASSES, M], U8, "w4_planes")
         nc.vector.memset(w4_planes[:].bitcast(I32), 0)
         v_planes = kept([P, PASSES * S], U8, "v_planes")
         nc.vector.memset(v_planes[:].bitcast(I32), 0)
-        b_rows = kept([P, P], F32, "b_rows")
-        nc.vector.memset(b_rows[:], 0.0)
         for q in range(QUADS):
             nc.gpsimd.dma_start(
                 w4_planes[32 * q : 32 * q + 4, :, :].bitcast(I32),
                 w4_scales[:, 4 * q : 4 * q + 4, :].rearrange("a r n -> r a n").bitcast(I32),
             )
-        nc.gpsimd.dma_start(b_rows[0:ROW_TILES, :], b.rearrange("(i p) -> i p", p=P))
-        identity = kept([P, P], F32, "identity")
-        make_identity(nc, identity[:])
         b_bank = psum_b.tile([P, P], F32, name="b_bank")
         nc.tensor.transpose(b_bank[:], b_rows[:], identity[:])
         bias = kept([P, ROW_TILES], F32, "bias")
@@ -99,25 +107,28 @@ def tile_list_tabgate_gelu_kernel(
         nc.vector.tensor_copy(picked_scales[:], scale_rows[:].indirect(offsets[:]))
         for a in range(PASSES):
             for q in range(QUADS):
-                row = 16 * a + 4 * q
+                row = 4 * (16 * a + 4 * q)
                 nc.gpsimd.dma_start(
                     v_planes[32 * q : 32 * q + 4, a * S : (a + 1) * S].bitcast(I32),
-                    picked_scales[row : row + 4, :].bitcast(I32),
+                    picked_scales[row : row + 13 : 4, :].bitcast(I32),
                 )
 
-        down_codes, down_planes = [], []
+        def quantise(grouped, width, name):
+            codes = kept([P, width], U32, name + "_codes")
+            plane = kept([P, width], U8, name + "_plane")
+            nc.vector.quantize_mx(out=codes[:].bitcast(FP8X4), scales=plane[:], in_=grouped)
+            return codes, plane
+
+        down_mx = []
         for a in range(PASSES):
             grouped = kept([P, PACK * R], BF16, "down_grouped%d" % a)
             nc.scalar.copy(
                 grouped[:].rearrange("p (t m j) -> p m j t", t=PACK, j=PACK),
                 down_raw[:, a, :].rearrange("p (j m t) -> p m j t", t=PACK, j=PACK),
             )
-            codes = kept([P, R], U32, "down_codes%d" % a)
-            plane = kept([P, R], U8, "down_plane%d" % a)
-            nc.vector.quantize_mx(out=codes[:].bitcast(FP8X4), scales=plane[:], in_=grouped[:])
-            down_codes.append(codes)
-            down_planes.append(plane)
-        load_gates(4)
+            down_mx.append(quantise(grouped[:], R, "down%d" % a))
+        load_gates(1)
+        up_raw.append(load_up(1, kept([P, PACK * HALF], F32, "up_raw1", tag="down_grouped1")))
 
         def list_slice(c):
             return offsets[:, c * LIST_COLS : (c + 1) * LIST_COLS]
@@ -127,33 +138,38 @@ def tile_list_tabgate_gelu_kernel(
             for c in range(CHUNKS):
                 picked[a, c] = kept([P, CHUNK], U32, "picked%d_%d" % (a, c))
                 nc.vector.tensor_copy(picked[a, c][:], table[a][:].bitcast(U32).indirect(list_slice(c)))
-            load_gates(5 + a)
+            load_gates(2 + a)
 
-        up_grouped = kept([P, PACK * M], BF16, "up_grouped")
-        nc.vector.tensor_copy(
-            up_grouped[:].rearrange("p (c i j) -> p c j i", i=4, j=PACK),
-            up_raw[:].rearrange("p (j c i) -> p c j i", i=4, j=PACK),
-        )
-        load_gates(7)
-        up_codes = kept([P, M], U32, "up_codes")
-        up_plane = kept([P, M], U8, "up_plane")
-        nc.vector.quantize_mx(out=up_codes[:].bitcast(FP8X4), scales=up_plane[:], in_=up_grouped[:])
+        up_mx = []
 
-        h_codes, h_planes = [], []
-        for c in range(CHUNKS):
-            grouped = kept([P, PACK * CHUNK], BF16, "h_grouped%d" % c)
+        def quantise_up(half, copy):
+            grouped = kept([P, PACK * HALF], BF16, "up_grouped%d" % half)
+            copy(
+                grouped[:].rearrange("p (c i j) -> p c j i", i=4, j=PACK),
+                up_raw[half][:].rearrange("p (j c i) -> p c j i", i=4, j=PACK),
+            )
+            up_mx.append(quantise(grouped[:], HALF, "up%d" % half))
+
+        quantise_up(0, nc.vector.tensor_copy)
+        load_gates(4)
+
+        h_mx = []
+        h_grouped = big_tile(5, [P, PACK * S], BF16, "h_grouped")
+
+        def make_h(c):
+            grouped = h_grouped[:, c * PACK * CHUNK : (c + 1) * PACK * CHUNK]
             for s in range(CHUNK // P):
                 bank = psum_h.tile([P, PACK, P], F32, name="h_bank")
-                cols = slice(s * P, (s + 1) * P)
+                first = c * CHUNK + s * P
                 for t in range(PACK):
                     for a in range(PASSES):
-                        first = a * S + c * CHUNK + s * P
+                        codes, plane = down_mx[a]
                         nc.tensor.matmul_mx(
                             out=bank[:, t, :],
-                            lhsT=down_codes[a][:, t * P : (t + 1) * P].bitcast(FP8X4),
-                            lhsT_scale=down_planes[a][:, t * P : (t + 1) * P],
-                            rhs=picked[a, c][:, cols].bitcast(FP8X4),
-                            rhs_scale=v_planes[:, first : first + P],
+                            lhsT=codes[:, t * P : (t + 1) * P].bitcast(FP8X4),
+                            lhsT_scale=plane[:, t * P : (t + 1) * P],
+                            rhs=picked[a, c][:, s * P : (s + 1) * P].bitcast(FP8X4),
+                            rhs_scale=v_planes[:, a * S + first : a * S + first + P],
                             start=(a == 0),
                             stop=(a == PASSES - 1),
                         )
@@ -161,43 +177,65 @@ def tile_list_tabgate_gelu_kernel(
                     grouped[:, s * PACK * P : (s + 1) * PACK * P].rearrange("p (j t) -> p j t", t=PACK),
                     bank[:].rearrange("p t j -> p j t"),
                 )
-            codes = kept([P, CHUNK], U32, "h_codes%d" % c)
-            plane = kept([P, CHUNK], U8, "h_plane%d" % c)
-            nc.vector.quantize_mx(out=codes[:].bitcast(FP8X4), scales=plane[:], in_=grouped[:])
-            h_codes.append(codes)
-            h_planes.append(plane)
+            h_mx.append(quantise(grouped, CHUNK, "h%d" % c))
 
-        for i in range(ROW_TILES):
+        def gated_chunk(i, c, result):
             rows = slice(i * P, (i + 1) * P)
-            if i < 2:
-                result = kept([P, S], F32, "result%d" % i)
-            else:
-                result = big_tile((4 + i - 2) % 8, [P, S], F32, "result%d" % i)
-            for c in range(CHUNKS):
-                bank = psum_y.tile([P, CHUNK], F32, name="y_bank")
-                for a in range(PASSES):
-                    first = a * S + c * CHUNK
-                    nc.tensor.matmul_mx(
-                        out=bank[:],
-                        lhsT=w4[:, a, 2 * i * P : 2 * (i + 1) * P].bitcast(FP4X4),
-                        lhsT_scale=w4_planes[:, a, rows],
-                        rhs=picked[a, c][:].bitcast(FP8X4),
-                        rhs_scale=v_planes[:, first : first + CHUNK],
-                        start=(a == 0),
-                        stop=False,
-                    )
+            bank = psum_y.tile([P, CHUNK], F32, name="y_bank")
+            for a in range(PASSES):
+                first = a * S + c * CHUNK
                 nc.tensor.matmul_mx(
                     out=bank[:],
-                    lhsT=up_codes[:, rows].bitcast(FP8X4),
-                    lhsT_scale=up_plane[:, rows],
-                    rhs=h_codes[c][:].bitcast(FP8X4),
-                    rhs_scale=h_planes[c][:],
-                    start=False,
-                    stop=True,
+                    lhsT=w4[:, a, 2 * i * P : 2 * (i + 1) * P].bitcast(FP4X4),
+                    lhsT_scale=w4_planes[:, a, rows],
+                    rhs=picked[a, c][:].bitcast(FP8X4),
+                    rhs_scale=v_planes[:, first : first + CHUNK],
+                    start=(a == 0),
+                    stop=False,
                 )
-                act = acts.tile([P, CHUNK], F32, name="act")
-                nc.scalar.activation(act[:], bank[:], gelu, bias=bias[:, i : i + 1])
-                nc.vector.tensor_tensor(
-                    result[:, c * CHUNK : (c + 1) * CHUNK], gates[i][:].indirect(list_slice(c)), act[:], mult
-                )
-            nc.sync.dma_start(out[rows, :], result[:])
+            half, column = divmod(i * P, HALF)
+            up_codes, up_plane = up_mx[half]
+            h_codes, h_plane = h_mx[c]
+            nc.tensor.matmul_mx(
+                out=bank[:],
+                lhsT=up_codes[:, column : column + P].bitcast(FP8X4),
+                lhsT_scale=up_plane[:, column : column + P],
+                rhs=h_codes[:].bitcast(FP8X4),
+                rhs_scale=h_plane[:],
+                start=False,
+                stop=True,
+            )
+            act = acts.tile([P, CHUNK], F32, name="act")
+            nc.scalar.activation(act[:], bank[:], gelu, bias=bias[:, i : i + 1])
+            nc.vector.tensor_tensor(result, gates[i][:].indirect(list_slice(c)), act[:], mult)
+
+        results = kept([P, ROW_TILES * S], F32, "results")
+
+        def store(first_tile, tiles, first_col, cols):
+            nc.sync.dma_start(
+                out[first_tile * P : (first_tile + tiles) * P, first_col : first_col + cols].rearrange(
+                    "(u p) s -> p u s", p=P
+                ),
+                results[:, first_tile * S : (first_tile + tiles) * S].rearrange("p (u s) -> p u s", u=tiles)[
+                    :, :, first_col : first_col + cols
+                ],
+            )
+
+        for i in range(ROW_TILES):
+            if i == 2:
+                quantise_up(1, nc.scalar.copy)
+            for c in range(CHUNKS):
+                if i == 0:
+                    make_h(c)
+                gated_chunk(i, c, results[:, i * S + c * CHUNK : i * S + (c + 1) * CHUNK])
+                if i == ROW_TILES - 1 and c == 1:
+                    store(i, 1, 0, 2 * CHUNK)
+            if i == 0:
+                load_gates(5)
+            if i + SLOTS < ROW_TILES:
+                load_gates(i + SLOTS)
+            if i in (1, 3, 5):
+                store(i - 1, 2, 0, S)
+            if i == 6:
+                store(i, 1, 0, S)
+        store(ROW_TILES - 1, 1, 2 * CHUNK, CHUNK)

@@ -59,14 +59,8 @@ def tile_list_tabgate_gelu_kernel(
             nc.sync.dma_start(words[:], tab_words[a].rearrange("p t i -> p (t i)").bitcast(I32))
             table.append(words)
 
-        def load_up(half, raw):
-            nc.sync.dma_start(
-                raw[:].rearrange("p (j n) -> p j n", j=PACK),
-                up[:, half * HALF : (half + 1) * HALF].rearrange("(p j) n -> p j n", j=PACK),
-            )
-            return raw
-
-        up_raw = [load_up(0, big_tile(4, [P, PACK * HALF], F32, "up_raw0"))]
+        up_raw = big_tile(4, [P, PACK * M], F32, "up_raw")
+        nc.sync.dma_start(up_raw[:], up.rearrange("(p j) n -> p (j n)", j=PACK))
         w4 = kept([P, PASSES, 2 * M], U8, "w4")
         nc.sync.dma_start(w4[:].bitcast(I32), w4_words.rearrange("a p n -> p a n").bitcast(I32))
 
@@ -93,10 +87,10 @@ def tile_list_tabgate_gelu_kernel(
         nc.vector.memset(w4_planes[:].bitcast(I32), 0)
         v_planes = kept([P, PASSES * S], U8, "v_planes")
         nc.vector.memset(v_planes[:].bitcast(I32), 0)
-        for q in range(QUADS):
+        for r in range(4):
             nc.gpsimd.dma_start(
-                w4_planes[32 * q : 32 * q + 4, :, :].bitcast(I32),
-                w4_scales[:, 4 * q : 4 * q + 4, :].rearrange("a r n -> r a n").bitcast(I32),
+                w4_planes[r:P:32, :, :].bitcast(I32),
+                w4_scales[:, r:16:4, :].rearrange("a q n -> q a n").bitcast(I32),
             )
         b_bank = psum_b.tile([P, P], F32, name="b_bank")
         nc.tensor.transpose(b_bank[:], b_rows[:], identity[:])
@@ -106,11 +100,11 @@ def tile_list_tabgate_gelu_kernel(
         picked_scales = kept([P, S], U8, "picked_scales")
         nc.vector.tensor_copy(picked_scales[:], scale_rows[:].indirect(offsets[:]))
         for a in range(PASSES):
-            for q in range(QUADS):
-                row = 4 * (16 * a + 4 * q)
+            for r in range(4):
+                first = 4 * (16 * a + r)
                 nc.gpsimd.dma_start(
-                    v_planes[32 * q : 32 * q + 4, a * S : (a + 1) * S].bitcast(I32),
-                    picked_scales[row : row + 13 : 4, :].bitcast(I32),
+                    v_planes[r:P:32, a * S : (a + 1) * S].bitcast(I32),
+                    picked_scales[first : first + 49 : 16, :].bitcast(I32),
                 )
 
         def quantise(grouped, width, name):
@@ -128,7 +122,6 @@ def tile_list_tabgate_gelu_kernel(
             )
             down_mx.append(quantise(grouped[:], R, "down%d" % a))
         load_gates(1)
-        up_raw.append(load_up(1, kept([P, PACK * HALF], F32, "up_raw1", tag="down_grouped1")))
 
         def list_slice(c):
             return offsets[:, c * LIST_COLS : (c + 1) * LIST_COLS]
@@ -146,11 +139,12 @@ def tile_list_tabgate_gelu_kernel(
             grouped = kept([P, PACK * HALF], BF16, "up_grouped%d" % half)
             copy(
                 grouped[:].rearrange("p (c i j) -> p c j i", i=4, j=PACK),
-                up_raw[half][:].rearrange("p (j c i) -> p c j i", i=4, j=PACK),
+                up_raw[:].rearrange("p (j u c i) -> p u c j i", i=4, j=PACK, u=2)[:, half],
             )
             up_mx.append(quantise(grouped[:], HALF, "up%d" % half))
 
         quantise_up(0, nc.vector.tensor_copy)
+        quantise_up(1, nc.vector.tensor_copy)
         load_gates(4)
 
         h_mx = []
@@ -222,8 +216,6 @@ def tile_list_tabgate_gelu_kernel(
             )
 
         for i in range(ROW_TILES):
-            if i == 2:
-                quantise_up(1, nc.scalar.copy)
             for c in range(CHUNKS):
                 if i == 0:
                     make_h(c)

@@ -24,8 +24,9 @@ LIST_COLS = CHUNK // 16
 ROW_TILES = M // P
 QUADS = 4
 ALIGN = 64
-SLOTS = 6
+RAW_FIRST = P - 16
 HALF = M // 2
+STORE_TILES = (4, 2, 2)
 
 
 def tile_list_tabgate_gelu_kernel(
@@ -37,75 +38,63 @@ def tile_list_tabgate_gelu_kernel(
 
     with ExitStack() as ctx:
         keep = ctx.enter_context(tc.tile_pool(name="keep", bufs=1))
-        big = ctx.enter_context(tc.tile_pool(name="big", bufs=1))
         acts = ctx.enter_context(tc.tile_pool(name="acts", bufs=6))
         psum_h = ctx.enter_context(tc.psum_pool(name="psum_h", bufs=3))
         psum_y = ctx.enter_context(tc.psum_pool(name="psum_y", bufs=4))
         psum_b = ctx.enter_context(tc.psum_pool(name="psum_b", bufs=1))
 
-        def big_tile(slot, shape, dtype, name):
-            return big.tile(shape, dtype, name=name, tag="slot%d" % slot, align_bytes=ALIGN)
-
         def kept(shape, dtype, name, tag=None):
             return keep.tile(shape, dtype, name=name, tag=tag or name, align_bytes=ALIGN)
 
+        down_raw = []
+
+        def load_down(a, tag):
+            raw = kept([P, PACK * R], F32, "down_raw%d" % a, tag)
+            nc.sync.dma_start(raw[:], down.rearrange("(a p j) r -> a p (j r)", a=PASSES, j=PACK)[a])
+            down_raw.append(raw)
+
+        load_down(0, None)
         offsets = keep.tile([P, S // 16], U16, name="offsets")
         nc.sync.dma_start(offsets[:], offs)
-        down_raw = big_tile(1, [P, PASSES, PACK * R], F32, "down_raw")
-        nc.sync.dma_start(down_raw[:], down.rearrange("(a p j) r -> p a (j r)", a=PASSES, j=PACK))
+        scale_rows = kept([P, PASSES * T], U8, "scale_rows")
+        nc.vector.memset(scale_rows[0:RAW_FIRST, :].bitcast(I32), 0)
+        nc.sync.dma_start(
+            scale_rows[RAW_FIRST:P, :].bitcast(I32).rearrange("q (a t) -> q a t", a=PASSES),
+            tab_scales.rearrange("a q t -> q a t").bitcast(I32),
+        )
+        w4_planes = kept([P, PASSES, M], U8, "w4_planes")
+        nc.gpsimd.memset(w4_planes[:].bitcast(I32), 0)
+        for r in range(4):
+            nc.sync.dma_start(
+                w4_planes[r:P:32, :, :].bitcast(I32),
+                w4_scales[:, r:16:4, :].rearrange("a q n -> q a n").bitcast(I32),
+            )
+        load_down(1, "slot_up")
         table = []
         for a in range(PASSES):
-            words = big_tile(2 + a, [P, T], I32, "table%d" % a)
+            words = kept([P, T], I32, "table%d" % a, "slot_table%d" % a)
             nc.sync.dma_start(words[:], tab_words[a].rearrange("p t i -> p (t i)").bitcast(I32))
             table.append(words)
 
-        up_raw = big_tile(4, [P, PACK * M], F32, "up_raw")
-        nc.sync.dma_start(up_raw[:], up.rearrange("(p j) n -> p (j n)", j=PACK))
-        w4 = kept([P, PASSES, 2 * M], U8, "w4")
-        nc.sync.dma_start(w4[:].bitcast(I32), w4_words.rearrange("a p n -> p a n").bitcast(I32))
-
-        gates = []
-
-        def load_gates(i):
-            g = big_tile(i % SLOTS, [P, T], F32, "gates%d" % i)
-            nc.sync.dma_start(g[:], gT[i * P : (i + 1) * P, :])
-            gates.append(g)
-
-        load_gates(0)
-
-        scale_rows = kept([P, T], U8, "scale_rows")
-        nc.vector.memset(scale_rows[:].bitcast(I32), 0)
-        nc.scalar.dma_start(
-            scale_rows[0:P:4, :].bitcast(I32), tab_scales.rearrange("a q t -> (a q) t").bitcast(I32)
-        )
         b_rows = kept([P, P], F32, "b_rows")
         nc.gpsimd.memset(b_rows[:], 0.0)
         nc.gpsimd.dma_start(b_rows[0:ROW_TILES, :], b.rearrange("(i p) -> i p", p=P))
         identity = kept([P, P], F32, "identity")
         make_identity(nc, identity[:])
-        w4_planes = kept([P, PASSES, M], U8, "w4_planes")
-        nc.vector.memset(w4_planes[:].bitcast(I32), 0)
-        v_planes = kept([P, PASSES * S], U8, "v_planes")
-        nc.vector.memset(v_planes[:].bitcast(I32), 0)
-        for r in range(4):
-            nc.gpsimd.dma_start(
-                w4_planes[r:P:32, :, :].bitcast(I32),
-                w4_scales[:, r:16:4, :].rearrange("a q n -> q a n").bitcast(I32),
-            )
         b_bank = psum_b.tile([P, P], F32, name="b_bank")
         nc.tensor.transpose(b_bank[:], b_rows[:], identity[:])
         bias = kept([P, ROW_TILES], F32, "bias")
         nc.scalar.copy(bias[:], b_bank[:, 0:ROW_TILES])
 
-        picked_scales = kept([P, S], U8, "picked_scales")
-        nc.vector.tensor_copy(picked_scales[:], scale_rows[:].indirect(offsets[:]))
+        v_planes = kept([P, PASSES * S], U8, "v_planes")
+        nc.vector.memset(v_planes[:].bitcast(I32), 0)
+        picked_scales = kept([P, PASSES * S], U8, "picked_scales")
         for a in range(PASSES):
-            for r in range(4):
-                first = 4 * (16 * a + r)
-                nc.gpsimd.dma_start(
-                    v_planes[r:P:32, a * S : (a + 1) * S].bitcast(I32),
-                    picked_scales[first : first + 49 : 16, :].bitcast(I32),
-                )
+            nc.vector.tensor_copy(
+                picked_scales[:, a * S : (a + 1) * S], scale_rows[:, a * T : (a + 1) * T].indirect(offsets[:])
+            )
+        for r in range(4):
+            nc.sync.dma_start(v_planes[r:P:32, :].bitcast(I32), picked_scales[RAW_FIRST + r : P : 4, :].bitcast(I32))
 
         def quantise(grouped, width, name):
             codes = kept([P, width], U32, name + "_codes")
@@ -115,13 +104,25 @@ def tile_list_tabgate_gelu_kernel(
 
         down_mx = []
         for a in range(PASSES):
-            grouped = kept([P, PACK * R], BF16, "down_grouped%d" % a)
+            grouped = kept([P, PACK * R], BF16, "down_grouped%d" % a, "slot_w4" if a else None)
             nc.scalar.copy(
                 grouped[:].rearrange("p (t m j) -> p m j t", t=PACK, j=PACK),
-                down_raw[:, a, :].rearrange("p (j m t) -> p m j t", t=PACK, j=PACK),
+                down_raw[a][:].rearrange("p (j m t) -> p m j t", t=PACK, j=PACK),
             )
             down_mx.append(quantise(grouped[:], R, "down%d" % a))
-        load_gates(1)
+
+        up_raw = kept([P, PACK * M], F32, "up_raw", "slot_up")
+        nc.sync.dma_start(up_raw[:], up.rearrange("(p j) n -> p (j n)", j=PACK))
+        w4 = kept([P, PASSES, 2 * M], U8, "w4", "slot_w4")
+        nc.sync.dma_start(w4[:].bitcast(I32), w4_words.rearrange("a p n -> p a n").bitcast(I32))
+
+        gates = []
+        gate_slots = ["slot_table0", "slot_table1", "slot_h", "slot_up", "slot_up_grouped"]
+
+        def load_gates(i):
+            g = kept([P, T], F32, "gates%d" % i, gate_slots[i % len(gate_slots)])
+            nc.sync.dma_start(g[:], gT[i * P : (i + 1) * P, :])
+            gates.append(g)
 
         def list_slice(c):
             return offsets[:, c * LIST_COLS : (c + 1) * LIST_COLS]
@@ -131,27 +132,12 @@ def tile_list_tabgate_gelu_kernel(
             for c in range(CHUNKS):
                 picked[a, c] = kept([P, CHUNK], U32, "picked%d_%d" % (a, c))
                 nc.vector.tensor_copy(picked[a, c][:], table[a][:].bitcast(U32).indirect(list_slice(c)))
-            load_gates(2 + a)
-
-        up_mx = []
-
-        def quantise_up(half, copy):
-            grouped = kept([P, PACK * HALF], BF16, "up_grouped%d" % half)
-            copy(
-                grouped[:].rearrange("p (c i j) -> p c j i", i=4, j=PACK),
-                up_raw[:].rearrange("p (j u c i) -> p u c j i", i=4, j=PACK, u=2)[:, half],
-            )
-            up_mx.append(quantise(grouped[:], HALF, "up%d" % half))
-
-        quantise_up(0, nc.vector.tensor_copy)
-        quantise_up(1, nc.vector.tensor_copy)
-        load_gates(4)
+            load_gates(a)
 
         h_mx = []
-        h_grouped = big_tile(5, [P, PACK * S], BF16, "h_grouped")
 
         def make_h(c):
-            grouped = h_grouped[:, c * PACK * CHUNK : (c + 1) * PACK * CHUNK]
+            grouped = kept([P, PACK * CHUNK], BF16, "h_grouped%d" % c, None if c else "slot_h")
             for s in range(CHUNK // P):
                 bank = psum_h.tile([P, PACK, P], F32, name="h_bank")
                 first = c * CHUNK + s * P
@@ -171,7 +157,21 @@ def tile_list_tabgate_gelu_kernel(
                     grouped[:, s * PACK * P : (s + 1) * PACK * P].rearrange("p (j t) -> p j t", t=PACK),
                     bank[:].rearrange("p t j -> p j t"),
                 )
-            h_mx.append(quantise(grouped, CHUNK, "h%d" % c))
+            h_mx.append(quantise(grouped[:], CHUNK, "h%d" % c))
+
+        make_h(0)
+        load_gates(2)
+
+        up_mx = []
+        for half in range(2):
+            grouped = kept([P, PACK * HALF], BF16, "up_grouped%d" % half, "slot_up_grouped" if half else None)
+            nc.vector.tensor_copy(
+                grouped[:].rearrange("p (c i j) -> p c j i", i=4, j=PACK),
+                up_raw[:].rearrange("p (j u c i) -> p u c j i", i=4, j=PACK, u=2)[:, half],
+            )
+            up_mx.append(quantise(grouped[:], HALF, "up%d" % half))
+        load_gates(3)
+        load_gates(4)
 
         def gated_chunk(i, c, result):
             rows = slice(i * P, (i + 1) * P)
@@ -203,31 +203,19 @@ def tile_list_tabgate_gelu_kernel(
             nc.scalar.activation(act[:], bank[:], gelu, bias=bias[:, i : i + 1])
             nc.vector.tensor_tensor(result, gates[i][:].indirect(list_slice(c)), act[:], mult)
 
-        results = kept([P, ROW_TILES * S], F32, "results")
-
-        def store(first_tile, tiles, first_col, cols):
+        first_tile = 0
+        for tiles in STORE_TILES:
+            results = kept([P, tiles * S], F32, "results%d" % first_tile)
+            for u in range(tiles):
+                i = first_tile + u
+                for c in range(CHUNKS):
+                    if i == 0 and c > 0:
+                        make_h(c)
+                    gated_chunk(i, c, results[:, u * S + c * CHUNK : u * S + (c + 1) * CHUNK])
+                if len(gates) < ROW_TILES:
+                    load_gates(len(gates))
             nc.sync.dma_start(
-                out[first_tile * P : (first_tile + tiles) * P, first_col : first_col + cols].rearrange(
-                    "(u p) s -> p u s", p=P
-                ),
-                results[:, first_tile * S : (first_tile + tiles) * S].rearrange("p (u s) -> p u s", u=tiles)[
-                    :, :, first_col : first_col + cols
-                ],
+                out[first_tile * P : (first_tile + tiles) * P, :].rearrange("(u p) s -> p u s", p=P),
+                results[:].rearrange("p (u s) -> p u s", u=tiles),
             )
-
-        for i in range(ROW_TILES):
-            for c in range(CHUNKS):
-                if i == 0:
-                    make_h(c)
-                gated_chunk(i, c, results[:, i * S + c * CHUNK : i * S + (c + 1) * CHUNK])
-                if i == ROW_TILES - 1 and c == 1:
-                    store(i, 1, 0, 2 * CHUNK)
-            if i == 0:
-                load_gates(5)
-            if i + SLOTS < ROW_TILES:
-                load_gates(i + SLOTS)
-            if i in (1, 3, 5):
-                store(i - 1, 2, 0, S)
-            if i == 6:
-                store(i, 1, 0, S)
-        store(ROW_TILES - 1, 1, 2 * CHUNK, CHUNK)
+            first_tile = first_tile + tiles

@@ -1,7 +1,6 @@
 from contextlib import ExitStack
 
 import concourse.mybir as mybir
-from concourse.masks import make_identity
 
 K, M, T, S, R = 1024, 1024, 4096, 1536, 512
 FLOPS = 2 * S * (K * R + K * M + R * M)
@@ -18,15 +17,20 @@ FP4X4 = mybir.dt.float4_e2m1fn_x4
 P = 128
 PACK = 4
 PASSES = K // (P * PACK)
+BLOCKS = 16
+QUADRANT = 32
+PLANE_ROWS = 4
+ROW_STEP = P // (PASSES * BLOCKS)
 CHUNK = 512
 CHUNKS = S // CHUNK
 LIST_COLS = CHUNK // 16
 ROW_TILES = M // P
-QUADS = 4
+HALVES = 2
+HALF_TILES = ROW_TILES // HALVES
 ALIGN = 64
-RAW_FIRST = P - 16
-HALF = M // 2
-STORE_TILES = (4, 2, 2)
+ACT_BUFS = 2 * CHUNKS
+H_BANKS, Y_BANKS = 4, 4
+STORE_TILES = (5, 2, 1)
 
 
 def tile_list_tabgate_gelu_kernel(
@@ -38,10 +42,9 @@ def tile_list_tabgate_gelu_kernel(
 
     with ExitStack() as ctx:
         keep = ctx.enter_context(tc.tile_pool(name="keep", bufs=1))
-        acts = ctx.enter_context(tc.tile_pool(name="acts", bufs=6))
-        psum_h = ctx.enter_context(tc.psum_pool(name="psum_h", bufs=3))
-        psum_y = ctx.enter_context(tc.psum_pool(name="psum_y", bufs=4))
-        psum_b = ctx.enter_context(tc.psum_pool(name="psum_b", bufs=1))
+        acts = ctx.enter_context(tc.tile_pool(name="acts", bufs=ACT_BUFS))
+        psum_h = ctx.enter_context(tc.psum_pool(name="psum_h", bufs=H_BANKS))
+        psum_y = ctx.enter_context(tc.psum_pool(name="psum_y", bufs=Y_BANKS))
 
         def kept(shape, dtype, name, tag=None):
             return keep.tile(shape, dtype, name=name, tag=tag or name, align_bytes=ALIGN)
@@ -53,48 +56,52 @@ def tile_list_tabgate_gelu_kernel(
             nc.sync.dma_start(raw[:], down.rearrange("(a p j) r -> a p (j r)", a=PASSES, j=PACK)[a])
             down_raw.append(raw)
 
-        load_down(0, None)
+        load_down(0, "slot_up")
         offsets = keep.tile([P, S // 16], U16, name="offsets")
         nc.sync.dma_start(offsets[:], offs)
-        scale_rows = kept([P, PASSES * T], U8, "scale_rows")
-        nc.vector.memset(scale_rows[0:RAW_FIRST, :].bitcast(I32), 0)
+        bias = kept([P, ROW_TILES], F32, "bias")
+        nc.sync.dma_start(bias[:], b.rearrange("(p i) -> p i", i=ROW_TILES))
+        scale_rows = kept([P, T], U8, "scale_rows", "slot_table1")
+        nc.gpsimd.memset(scale_rows[:, 0 : T // 2].bitcast(I32), 0)
+        nc.vector.memset(scale_rows[:, T // 2 : T].bitcast(I32), 0)
         nc.sync.dma_start(
-            scale_rows[RAW_FIRST:P, :].bitcast(I32).rearrange("q (a t) -> q a t", a=PASSES),
-            tab_scales.rearrange("a q t -> q a t").bitcast(I32),
+            scale_rows[0:P:ROW_STEP, :].bitcast(I32), tab_scales.rearrange("a q t -> (a q) t").bitcast(I32)
         )
-        w4_planes = kept([P, PASSES, M], U8, "w4_planes")
-        nc.gpsimd.memset(w4_planes[:].bitcast(I32), 0)
-        for r in range(4):
-            nc.sync.dma_start(
-                w4_planes[r:P:32, :, :].bitcast(I32),
-                w4_scales[:, r:16:4, :].rearrange("a q n -> q a n").bitcast(I32),
+        w4_rows = kept([P, PASSES, M], U8, "w4_rows", "slot_w4_rows")
+        nc.gpsimd.memset(w4_rows[:].bitcast(I32), 0)
+        for e in range(PLANE_ROWS):
+            nc.gpsimd.dma_start(
+                w4_rows[e:P:QUADRANT, :, :].bitcast(I32),
+                w4_scales[:, e:BLOCKS:PLANE_ROWS, :].rearrange("a q n -> q a n").bitcast(I32),
             )
-        load_down(1, "slot_up")
+        load_down(1, None)
         table = []
-        for a in range(PASSES):
+
+        def load_table(a):
             words = kept([P, T], I32, "table%d" % a, "slot_table%d" % a)
-            nc.sync.dma_start(words[:], tab_words[a].rearrange("p t i -> p (t i)").bitcast(I32))
+            nc.sync.dma_start(words[:], tab_words[a].rearrange("p t j -> p (t j)").bitcast(I32))
             table.append(words)
 
-        b_rows = kept([P, P], F32, "b_rows")
-        nc.gpsimd.memset(b_rows[:], 0.0)
-        nc.gpsimd.dma_start(b_rows[0:ROW_TILES, :], b.rearrange("(i p) -> i p", p=P))
-        identity = kept([P, P], F32, "identity")
-        make_identity(nc, identity[:])
-        b_bank = psum_b.tile([P, P], F32, name="b_bank")
-        nc.tensor.transpose(b_bank[:], b_rows[:], identity[:])
-        bias = kept([P, ROW_TILES], F32, "bias")
-        nc.scalar.copy(bias[:], b_bank[:, 0:ROW_TILES])
+        load_table(0)
+        w4_raw = kept([P, PASSES, 2 * M], U8, "w4_raw", "slot_w4_raw")
+        nc.sync.dma_start(w4_raw[:].bitcast(I32), w4_words.rearrange("a p n -> p a n").bitcast(I32))
 
         v_planes = kept([P, PASSES * S], U8, "v_planes")
         nc.vector.memset(v_planes[:].bitcast(I32), 0)
-        picked_scales = kept([P, PASSES * S], U8, "picked_scales")
-        for a in range(PASSES):
-            nc.vector.tensor_copy(
-                picked_scales[:, a * S : (a + 1) * S], scale_rows[:, a * T : (a + 1) * T].indirect(offsets[:])
-            )
-        for r in range(4):
-            nc.sync.dma_start(v_planes[r:P:32, :].bitcast(I32), picked_scales[RAW_FIRST + r : P : 4, :].bitcast(I32))
+        picked_scales = kept([P, S], U8, "picked_scales")
+        nc.vector.tensor_copy(picked_scales[:], scale_rows[:].indirect(offsets[:]))
+
+        def move_scales(a):
+            rows = picked_scales[a * BLOCKS * ROW_STEP : (a + 1) * BLOCKS * ROW_STEP, :]
+            for e in range(PLANE_ROWS):
+                nc.sync.dma_start(
+                    v_planes[e:P:QUADRANT, a * S : (a + 1) * S].bitcast(I32),
+                    rows[e * ROW_STEP :: PLANE_ROWS * ROW_STEP, :].bitcast(I32),
+                )
+
+        move_scales(0)
+        load_table(1)
+        move_scales(1)
 
         def quantise(grouped, width, name):
             codes = kept([P, width], U32, name + "_codes")
@@ -104,7 +111,7 @@ def tile_list_tabgate_gelu_kernel(
 
         down_mx = []
         for a in range(PASSES):
-            grouped = kept([P, PACK * R], BF16, "down_grouped%d" % a, "slot_w4" if a else None)
+            grouped = kept([P, PACK * R], BF16, "down_grouped%d" % a, "slot_down_grouped%d" % a)
             nc.scalar.copy(
                 grouped[:].rearrange("p (t m j) -> p m j t", t=PACK, j=PACK),
                 down_raw[a][:].rearrange("p (j m t) -> p m j t", t=PACK, j=PACK),
@@ -113,31 +120,42 @@ def tile_list_tabgate_gelu_kernel(
 
         up_raw = kept([P, PACK * M], F32, "up_raw", "slot_up")
         nc.sync.dma_start(up_raw[:], up.rearrange("(p j) n -> p (j n)", j=PACK))
-        w4 = kept([P, PASSES, 2 * M], U8, "w4", "slot_w4")
-        nc.sync.dma_start(w4[:].bitcast(I32), w4_words.rearrange("a p n -> p a n").bitcast(I32))
 
         gates = []
-        gate_slots = ["slot_table0", "slot_table1", "slot_h", "slot_up", "slot_up_grouped"]
+        gate_slots = ["slot_w4_rows", "slot_table0", "slot_w4_raw", "slot_table1", "slot_up", "slot_up_grouped"]
 
-        def load_gates(i):
+        def load_gates():
+            i = len(gates)
             g = kept([P, T], F32, "gates%d" % i, gate_slots[i % len(gate_slots)])
-            nc.sync.dma_start(g[:], gT[i * P : (i + 1) * P, :])
+            nc.sync.dma_start(g[:], gT.rearrange("(p i) t -> i p t", i=ROW_TILES)[i])
             gates.append(g)
 
         def list_slice(c):
             return offsets[:, c * LIST_COLS : (c + 1) * LIST_COLS]
 
+        def deal(dealt, raw):
+            nc.vector.tensor_copy(
+                dealt.rearrange("p a (u i m) -> p a u m i", u=HALVES, i=HALF_TILES),
+                raw.rearrange("p a (m u i) -> p a u m i", u=HALVES, i=HALF_TILES),
+            )
+
+        w4 = kept([P, PASSES, 2 * M], U8, "w4")
+        w4_planes = kept([P, PASSES, M], U8, "w4_planes", "slot_down_grouped1")
         picked = {}
         for a in range(PASSES):
             for c in range(CHUNKS):
                 picked[a, c] = kept([P, CHUNK], U32, "picked%d_%d" % (a, c))
                 nc.vector.tensor_copy(picked[a, c][:], table[a][:].bitcast(U32).indirect(list_slice(c)))
-            load_gates(a)
+            if a == 0:
+                deal(w4_planes[:], w4_rows[:])
+                deal(w4[:].bitcast(U16), w4_raw[:].bitcast(U16))
+        while gate_slots[len(gates)] != "slot_up":
+            load_gates()
 
         h_mx = []
 
         def make_h(c):
-            grouped = kept([P, PACK * CHUNK], BF16, "h_grouped%d" % c, None if c else "slot_h")
+            grouped = kept([P, PACK * CHUNK], BF16, "h_grouped%d" % c)
             for s in range(CHUNK // P):
                 bank = psum_h.tile([P, PACK, P], F32, name="h_bank")
                 first = c * CHUNK + s * P
@@ -160,34 +178,32 @@ def tile_list_tabgate_gelu_kernel(
             h_mx.append(quantise(grouped[:], CHUNK, "h%d" % c))
 
         make_h(0)
-        load_gates(2)
 
         up_mx = []
-        for half in range(2):
-            grouped = kept([P, PACK * HALF], BF16, "up_grouped%d" % half, "slot_up_grouped" if half else None)
+        for half in range(HALVES):
+            grouped = kept([P, PACK * HALF_TILES * P], BF16, "up_grouped%d" % half, "slot_up_grouped" if half else None)
             nc.vector.tensor_copy(
-                grouped[:].rearrange("p (c i j) -> p c j i", i=4, j=PACK),
-                up_raw[:].rearrange("p (j u c i) -> p u c j i", i=4, j=PACK, u=2)[:, half],
+                grouped[:].rearrange("p (i m j) -> p m j i", i=HALF_TILES, j=PACK),
+                up_raw[:].rearrange("p (j m u i) -> p u m j i", i=HALF_TILES, j=PACK, u=HALVES)[:, half],
             )
-            up_mx.append(quantise(grouped[:], HALF, "up%d" % half))
-        load_gates(3)
-        load_gates(4)
+            up_mx.append(quantise(grouped[:], HALF_TILES * P, "up%d" % half))
+        load_gates()
+        load_gates()
 
         def gated_chunk(i, c, result):
             rows = slice(i * P, (i + 1) * P)
             bank = psum_y.tile([P, CHUNK], F32, name="y_bank")
             for a in range(PASSES):
-                first = a * S + c * CHUNK
                 nc.tensor.matmul_mx(
                     out=bank[:],
                     lhsT=w4[:, a, 2 * i * P : 2 * (i + 1) * P].bitcast(FP4X4),
                     lhsT_scale=w4_planes[:, a, rows],
                     rhs=picked[a, c][:].bitcast(FP8X4),
-                    rhs_scale=v_planes[:, first : first + CHUNK],
+                    rhs_scale=v_planes[:, a * S + c * CHUNK : a * S + (c + 1) * CHUNK],
                     start=(a == 0),
                     stop=False,
                 )
-            half, column = divmod(i * P, HALF)
+            half, column = divmod(i * P, HALF_TILES * P)
             up_codes, up_plane = up_mx[half]
             h_codes, h_plane = h_mx[c]
             nc.tensor.matmul_mx(
@@ -209,13 +225,13 @@ def tile_list_tabgate_gelu_kernel(
             for u in range(tiles):
                 i = first_tile + u
                 for c in range(CHUNKS):
-                    if i == 0 and c > 0:
+                    if c == len(h_mx):
                         make_h(c)
                     gated_chunk(i, c, results[:, u * S + c * CHUNK : u * S + (c + 1) * CHUNK])
                 if len(gates) < ROW_TILES:
-                    load_gates(len(gates))
+                    load_gates()
             nc.sync.dma_start(
-                out[first_tile * P : (first_tile + tiles) * P, :].rearrange("(u p) s -> p u s", p=P),
-                results[:].rearrange("p (u s) -> p u s", u=tiles),
+                out.rearrange("(p i) s -> p (i s)", i=ROW_TILES)[:, first_tile * S : (first_tile + tiles) * S],
+                results[:],
             )
             first_tile = first_tile + tiles

@@ -27,7 +27,7 @@ LIST_COLS = CHUNK // 16
 ROW_TILES = M // P
 HALVES = 2
 HALF_TILES = ROW_TILES // HALVES
-ALIGN = 64
+ALIGN = 256
 ACT_BUFS = 2 * CHUNKS
 H_BANKS, Y_BANKS = 4, 4
 STORE_TILES = (5, 2, 1)
@@ -57,7 +57,7 @@ def tile_list_tabgate_gelu_kernel(
             down_raw.append(raw)
 
         load_down(0, "slot_up")
-        offsets = keep.tile([P, S // 16], U16, name="offsets")
+        offsets = kept([P, S // 16], U16, "offsets")
         nc.sync.dma_start(offsets[:], offs)
         bias = kept([P, ROW_TILES], F32, "bias")
         nc.sync.dma_start(bias[:], b.rearrange("(p i) -> p i", i=ROW_TILES))

@@ -1,6 +1,7 @@
 from contextlib import ExitStack
 
 import concourse.mybir as mybir
+from concourse.masks import make_identity
 
 K, M, T, S, R = 1024, 1024, 4096, 1536, 512
 FLOPS = 2 * S * (K * R + K * M + R * M)
@@ -21,6 +22,7 @@ BLOCKS = 16
 QUADRANT = 32
 PLANE_ROWS = 4
 ROW_STEP = P // (PASSES * BLOCKS)
+BIAS_ROW = 12
 CHUNK = 512
 CHUNKS = S // CHUNK
 LIST_COLS = CHUNK // 16
@@ -59,14 +61,15 @@ def tile_list_tabgate_gelu_kernel(
         load_down(0, "slot_up")
         offsets = kept([P, S // 16], U16, "offsets")
         nc.sync.dma_start(offsets[:], offs)
-        bias = kept([P, ROW_TILES], F32, "bias")
-        nc.sync.dma_start(bias[:], b.rearrange("(p i) -> p i", i=ROW_TILES))
         scale_rows = kept([P, T], U8, "scale_rows", "slot_table1")
         nc.gpsimd.memset(scale_rows[:, 0 : T // 2].bitcast(I32), 0)
         nc.vector.memset(scale_rows[:, T // 2 : T].bitcast(I32), 0)
         nc.sync.dma_start(
             scale_rows[0:P:ROW_STEP, :].bitcast(I32), tab_scales.rearrange("a q t -> (a q) t").bitcast(I32)
         )
+        bias_row = kept([P, M], F32, "bias_row", "h_grouped0")
+        nc.vector.memset(bias_row[:], 0.0)
+        nc.sync.dma_start(bias_row[BIAS_ROW : BIAS_ROW + 1, :], b.rearrange("(o n) -> o n", o=1))
         w4_rows = kept([P, PASSES, M], U8, "w4_rows", "slot_w4_rows")
         nc.gpsimd.memset(w4_rows[:].bitcast(I32), 0)
         for e in range(PLANE_ROWS):
@@ -74,6 +77,15 @@ def tile_list_tabgate_gelu_kernel(
                 w4_rows[e:P:QUADRANT, :, :].bitcast(I32),
                 w4_scales[:, e:BLOCKS:PLANE_ROWS, :].rearrange("a q n -> q a n").bitcast(I32),
             )
+        identity = kept([P, P], F32, "identity")
+        make_identity(nc, identity[:])
+        bias = kept([P, ROW_TILES], F32, "bias")
+        for half in range(HALVES):
+            bank = psum_y.tile([P, CHUNK], F32, name="y_bank")
+            for u in range(HALF_TILES):
+                i = half * HALF_TILES + u
+                nc.tensor.transpose(bank[:, u * P : (u + 1) * P], bias_row[:, i:M:ROW_TILES], identity[:])
+            nc.scalar.copy(bias[:, half * HALF_TILES : (half + 1) * HALF_TILES], bank[:, BIAS_ROW:CHUNK:P])
         load_down(1, None)
         table = []
 

@@ -1,7 +1,6 @@
 from contextlib import ExitStack
 
 import concourse.mybir as mybir
-from concourse.masks import make_identity
 
 K, M, T, S, R = 1024, 1024, 4096, 1536, 512
 FLOPS = 2 * S * (K * R + K * M + R * M)
@@ -21,8 +20,7 @@ PASSES = K // (P * PACK)
 BLOCKS = 16
 QUADRANT = 32
 PLANE_ROWS = 4
-ROW_STEP = P // (PASSES * BLOCKS)
-BIAS_ROW = 12
+ROW_FIRST, ROW_STEP = 0, 4
 CHUNK = 512
 CHUNKS = S // CHUNK
 LIST_COLS = CHUNK // 16
@@ -65,27 +63,16 @@ def tile_list_tabgate_gelu_kernel(
         nc.gpsimd.memset(scale_rows[:, 0 : T // 2].bitcast(I32), 0)
         nc.vector.memset(scale_rows[:, T // 2 : T].bitcast(I32), 0)
         nc.sync.dma_start(
-            scale_rows[0:P:ROW_STEP, :].bitcast(I32), tab_scales.rearrange("a q t -> (a q) t").bitcast(I32)
+            scale_rows[ROW_FIRST : ROW_FIRST + ROW_STEP * PASSES * BLOCKS : ROW_STEP, :].bitcast(I32),
+            tab_scales.rearrange("a q t -> (a q) t").bitcast(I32),
         )
-        bias_row = kept([P, M], F32, "bias_row", "h_grouped0")
-        nc.vector.memset(bias_row[:], 0.0)
-        nc.sync.dma_start(bias_row[BIAS_ROW : BIAS_ROW + 1, :], b.rearrange("(o n) -> o n", o=1))
         w4_rows = kept([P, PASSES, M], U8, "w4_rows", "slot_w4_rows")
         nc.gpsimd.memset(w4_rows[:].bitcast(I32), 0)
         for e in range(PLANE_ROWS):
-            nc.gpsimd.dma_start(
+            nc.scalar.dma_start(
                 w4_rows[e:P:QUADRANT, :, :].bitcast(I32),
                 w4_scales[:, e:BLOCKS:PLANE_ROWS, :].rearrange("a q n -> q a n").bitcast(I32),
             )
-        identity = kept([P, P], F32, "identity")
-        make_identity(nc, identity[:])
-        bias = kept([P, ROW_TILES], F32, "bias")
-        for half in range(HALVES):
-            bank = psum_y.tile([P, CHUNK], F32, name="y_bank")
-            for u in range(HALF_TILES):
-                i = half * HALF_TILES + u
-                nc.tensor.transpose(bank[:, u * P : (u + 1) * P], bias_row[:, i:M:ROW_TILES], identity[:])
-            nc.scalar.copy(bias[:, half * HALF_TILES : (half + 1) * HALF_TILES], bank[:, BIAS_ROW:CHUNK:P])
         load_down(1, None)
         table = []
 
@@ -104,11 +91,12 @@ def tile_list_tabgate_gelu_kernel(
         nc.vector.tensor_copy(picked_scales[:], scale_rows[:].indirect(offsets[:]))
 
         def move_scales(a):
-            rows = picked_scales[a * BLOCKS * ROW_STEP : (a + 1) * BLOCKS * ROW_STEP, :]
             for e in range(PLANE_ROWS):
+                first = ROW_FIRST + ROW_STEP * (a * BLOCKS + e)
+                step = ROW_STEP * PLANE_ROWS
                 nc.sync.dma_start(
                     v_planes[e:P:QUADRANT, a * S : (a + 1) * S].bitcast(I32),
-                    rows[e * ROW_STEP :: PLANE_ROWS * ROW_STEP, :].bitcast(I32),
+                    picked_scales[first : first + step * (P // QUADRANT - 1) + 1 : step, :].bitcast(I32),
                 )
 
         move_scales(0)
@@ -132,6 +120,8 @@ def tile_list_tabgate_gelu_kernel(
 
         up_raw = kept([P, PACK * M], F32, "up_raw", "slot_up")
         nc.sync.dma_start(up_raw[:], up.rearrange("(p j) n -> p (j n)", j=PACK))
+        bias = kept([P, ROW_TILES], F32, "bias")
+        nc.sync.dma_start(bias[:], b.rearrange("(p i) -> p i", i=ROW_TILES))
 
         gates = []
         gate_slots = ["slot_w4_rows", "slot_table0", "slot_w4_raw", "slot_table1", "slot_up", "slot_up_grouped"]
@@ -231,6 +221,7 @@ def tile_list_tabgate_gelu_kernel(
             nc.scalar.activation(act[:], bank[:], gelu, bias=bias[:, i : i + 1])
             nc.vector.tensor_tensor(result, gates[i][:].indirect(list_slice(c)), act[:], mult)
 
+        out_rows = out.rearrange("(p i) s -> p (i s)", i=ROW_TILES)
         first_tile = 0
         for tiles in STORE_TILES:
             results = kept([P, tiles * S], F32, "results%d" % first_tile)
@@ -242,8 +233,5 @@ def tile_list_tabgate_gelu_kernel(
                     gated_chunk(i, c, results[:, u * S + c * CHUNK : u * S + (c + 1) * CHUNK])
                 if len(gates) < ROW_TILES:
                     load_gates()
-            nc.sync.dma_start(
-                out.rearrange("(p i) s -> p (i s)", i=ROW_TILES)[:, first_tile * S : (first_tile + tiles) * S],
-                results[:],
-            )
+            nc.sync.dma_start(out_rows[:, first_tile * S : (first_tile + tiles) * S], results[:])
             first_tile = first_tile + tiles

@@ -56,6 +56,13 @@ def tile_list_tabgate_gelu_kernel(
             nc.sync.dma_start(raw[:], down.rearrange("(a p j) r -> a p (j r)", a=PASSES, j=PACK)[a])
             down_raw.append(raw)
 
+        w4_rows = kept([P, PASSES, M], U8, "w4_rows", "slot_w4_rows")
+        nc.gpsimd.memset(w4_rows[:].bitcast(I32), 0)
+        for e in range(PLANE_ROWS):
+            nc.scalar.dma_start(
+                w4_rows[e:P:QUADRANT, :, :].bitcast(I32),
+                w4_scales[:, e:BLOCKS:PLANE_ROWS, :].rearrange("a q n -> q a n").bitcast(I32),
+            )
         load_down(0, "slot_up")
         offsets = kept([P, S // 16], U16, "offsets")
         nc.sync.dma_start(offsets[:], offs)
@@ -66,13 +73,6 @@ def tile_list_tabgate_gelu_kernel(
             scale_rows[ROW_FIRST : ROW_FIRST + ROW_STEP * PASSES * BLOCKS : ROW_STEP, :].bitcast(I32),
             tab_scales.rearrange("a q t -> (a q) t").bitcast(I32),
         )
-        w4_rows = kept([P, PASSES, M], U8, "w4_rows", "slot_w4_rows")
-        nc.gpsimd.memset(w4_rows[:].bitcast(I32), 0)
-        for e in range(PLANE_ROWS):
-            nc.scalar.dma_start(
-                w4_rows[e:P:QUADRANT, :, :].bitcast(I32),
-                w4_scales[:, e:BLOCKS:PLANE_ROWS, :].rearrange("a q n -> q a n").bitcast(I32),
-            )
         load_down(1, None)
         table = []
 

@@ -1,6 +1,7 @@
 from contextlib import ExitStack
 
 import concourse.mybir as mybir
+from concourse.masks import make_identity
 
 K, M, T, S, R = 1024, 1024, 4096, 1536, 512
 FLOPS = 2 * S * (K * R + K * M + R * M)
@@ -21,6 +22,7 @@ BLOCKS = 16
 QUADRANT = 32
 PLANE_ROWS = 4
 ROW_FIRST, ROW_STEP = 0, 4
+BIAS_ROW = 12
 CHUNK = 512
 CHUNKS = S // CHUNK
 LIST_COLS = CHUNK // 16
@@ -30,7 +32,7 @@ HALF_TILES = ROW_TILES // HALVES
 ALIGN = 256
 ACT_BUFS = 2 * CHUNKS
 H_BANKS, Y_BANKS = 4, 4
-STORE_TILES = (5, 2, 1)
+STORE_TILES = (4, 3, 1)
 
 
 def tile_list_tabgate_gelu_kernel(
@@ -120,8 +122,18 @@ def tile_list_tabgate_gelu_kernel(
 
         up_raw = kept([P, PACK * M], F32, "up_raw", "slot_up")
         nc.sync.dma_start(up_raw[:], up.rearrange("(p j) n -> p (j n)", j=PACK))
+        bias_row = kept([P, M], F32, "bias_row", "h_grouped2")
+        nc.vector.memset(bias_row[:], 0.0)
+        nc.sync.dma_start(bias_row[BIAS_ROW : BIAS_ROW + 1, :], b.rearrange("(o n) -> o n", o=1))
+        identity = kept([P, P], F32, "identity")
+        make_identity(nc, identity[:])
         bias = kept([P, ROW_TILES], F32, "bias")
-        nc.sync.dma_start(bias[:], b.rearrange("(p i) -> p i", i=ROW_TILES))
+        for half in range(HALVES):
+            bank = psum_y.tile([P, CHUNK], F32, name="y_bank")
+            for u in range(HALF_TILES):
+                columns = slice(half * CHUNK + u, (half + 1) * CHUNK, HALF_TILES)
+                nc.tensor.transpose(bank[:, u * P : (u + 1) * P], bias_row[:, columns], identity[:])
+            nc.scalar.copy(bias[:, half * HALF_TILES : (half + 1) * HALF_TILES], bank[:, BIAS_ROW:CHUNK:P])
 
         gates = []
         gate_slots = ["slot_w4_rows", "slot_table0", "slot_w4_raw", "slot_table1", "slot_up", "slot_up_grouped"]
@@ -129,7 +141,7 @@ def tile_list_tabgate_gelu_kernel(
         def load_gates():
             i = len(gates)
             g = kept([P, T], F32, "gates%d" % i, gate_slots[i % len(gate_slots)])
-            nc.sync.dma_start(g[:], gT.rearrange("(p i) t -> i p t", i=ROW_TILES)[i])
+            nc.sync.dma_start(g[:], gT.rearrange("(u p i) t -> u i p t", u=HALVES, p=P)[i // HALF_TILES, i % HALF_TILES])
             gates.append(g)
 
         def list_slice(c):
@@ -138,7 +150,7 @@ def tile_list_tabgate_gelu_kernel(
         def deal(dealt, raw):
             nc.vector.tensor_copy(
                 dealt.rearrange("p a (u i m) -> p a u m i", u=HALVES, i=HALF_TILES),
-                raw.rearrange("p a (m u i) -> p a u m i", u=HALVES, i=HALF_TILES),
+                raw.rearrange("p a (u m i) -> p a u m i", u=HALVES, i=HALF_TILES),
             )
 
         w4 = kept([P, PASSES, 2 * M], U8, "w4")
@@ -186,7 +198,7 @@ def tile_list_tabgate_gelu_kernel(
             grouped = kept([P, PACK * HALF_TILES * P], BF16, "up_grouped%d" % half, "slot_up_grouped" if half else None)
             nc.vector.tensor_copy(
                 grouped[:].rearrange("p (i m j) -> p m j i", i=HALF_TILES, j=PACK),
-                up_raw[:].rearrange("p (j m u i) -> p u m j i", i=HALF_TILES, j=PACK, u=HALVES)[:, half],
+                up_raw[:].rearrange("p (j u m i) -> p u m j i", i=HALF_TILES, j=PACK, u=HALVES)[:, half],
             )
             up_mx.append(quantise(grouped[:], HALF_TILES * P, "up%d" % half))
         load_gates()
@@ -221,7 +233,7 @@ def tile_list_tabgate_gelu_kernel(
             nc.scalar.activation(act[:], bank[:], gelu, bias=bias[:, i : i + 1])
             nc.vector.tensor_tensor(result, gates[i][:].indirect(list_slice(c)), act[:], mult)
 
-        out_rows = out.rearrange("(p i) s -> p (i s)", i=ROW_TILES)
+        out_rows = out.rearrange("(u p i) s -> u p (i s)", u=HALVES, p=P)
         first_tile = 0
         for tiles in STORE_TILES:
             results = kept([P, tiles * S], F32, "results%d" % first_tile)
@@ -233,5 +245,6 @@ def tile_list_tabgate_gelu_kernel(
                     gated_chunk(i, c, results[:, u * S + c * CHUNK : u * S + (c + 1) * CHUNK])
                 if len(gates) < ROW_TILES:
                     load_gates()
-            nc.sync.dma_start(out_rows[:, first_tile * S : (first_tile + tiles) * S], results[:])
+            half, within = divmod(first_tile, HALF_TILES)
+            nc.sync.dma_start(out_rows[half, :, within * S : (within + tiles) * S], results[:])
             first_tile = first_tile + tiles

from contextlib import ExitStack

import concourse.mybir as mybir
from concourse.masks import make_identity

K, M, T, S, R = 1024, 1024, 4096, 1536, 512
FLOPS = 2 * S * (K * R + K * M + R * M)

F32 = mybir.dt.float32
BF16 = mybir.dt.bfloat16
I32 = mybir.dt.int32
U32 = mybir.dt.uint32
U16 = mybir.dt.uint16
U8 = mybir.dt.uint8
FP8X4 = mybir.dt.float8_e4m3fn_x4
FP4X4 = mybir.dt.float4_e2m1fn_x4

P = 128
PACK = 4
PASSES = K // (P * PACK)
BLOCKS = 16
QUADRANT = 32
PLANE_ROWS = 4
ROW_FIRST, ROW_STEP = 0, 4
BIAS_ROW = 12
CHUNK = 512
CHUNKS = S // CHUNK
LIST_COLS = CHUNK // 16
ROW_TILES = M // P
HALVES = 2
HALF_TILES = ROW_TILES // HALVES
ALIGN = 256
ACT_BUFS = 2 * CHUNKS
H_BANKS, Y_BANKS = 4, 4
STORE_TILES = (4, 3, 1)


def tile_list_tabgate_gelu_kernel(
    tc, tab_words, tab_scales, w4_words, w4_scales, down, up, gT, b, offs, out
):
    nc = tc.nc
    mult = mybir.AluOpType.mult
    gelu = mybir.ActivationFunctionType.Gelu_apprx_tanh

    with ExitStack() as ctx:
        keep = ctx.enter_context(tc.tile_pool(name="keep", bufs=1))
        acts = ctx.enter_context(tc.tile_pool(name="acts", bufs=ACT_BUFS))
        psum_h = ctx.enter_context(tc.psum_pool(name="psum_h", bufs=H_BANKS))
        psum_y = ctx.enter_context(tc.psum_pool(name="psum_y", bufs=Y_BANKS))

        def kept(shape, dtype, name, tag=None):
            return keep.tile(shape, dtype, name=name, tag=tag or name, align_bytes=ALIGN)

        down_raw = []

        def load_down(a, tag):
            raw = kept([P, PACK * R], F32, "down_raw%d" % a, tag)
            nc.sync.dma_start(raw[:], down.rearrange("(a p j) r -> a p (j r)", a=PASSES, j=PACK)[a])
            down_raw.append(raw)

        w4_rows = kept([P, PASSES, M], U8, "w4_rows", "slot_w4_rows")
        nc.gpsimd.memset(w4_rows[:].bitcast(I32), 0)
        for e in range(PLANE_ROWS):
            nc.scalar.dma_start(
                w4_rows[e:P:QUADRANT, :, :].bitcast(I32),
                w4_scales[:, e:BLOCKS:PLANE_ROWS, :].rearrange("a q n -> q a n").bitcast(I32),
            )
        load_down(0, "slot_up")
        offsets = kept([P, S // 16], U16, "offsets")
        nc.sync.dma_start(offsets[:], offs)
        scale_rows = kept([P, T], U8, "scale_rows", "slot_table1")
        nc.gpsimd.memset(scale_rows[:, 0 : T // 2].bitcast(I32), 0)
        nc.vector.memset(scale_rows[:, T // 2 : T].bitcast(I32), 0)
        nc.sync.dma_start(
            scale_rows[ROW_FIRST : ROW_FIRST + ROW_STEP * PASSES * BLOCKS : ROW_STEP, :].bitcast(I32),
            tab_scales.rearrange("a q t -> (a q) t").bitcast(I32),
        )
        load_down(1, None)
        table = []

        def load_table(a):
            words = kept([P, T], I32, "table%d" % a, "slot_table%d" % a)
            nc.sync.dma_start(words[:], tab_words[a].rearrange("p t j -> p (t j)").bitcast(I32))
            table.append(words)

        load_table(0)
        w4_raw = kept([P, PASSES, 2 * M], U8, "w4_raw", "slot_w4_raw")
        nc.sync.dma_start(w4_raw[:].bitcast(I32), w4_words.rearrange("a p n -> p a n").bitcast(I32))

        v_planes = kept([P, PASSES * S], U8, "v_planes")
        nc.vector.memset(v_planes[:].bitcast(I32), 0)
        picked_scales = kept([P, S], U8, "picked_scales")
        nc.vector.tensor_copy(picked_scales[:], scale_rows[:].indirect(offsets[:]))

        def move_scales(a):
            for e in range(PLANE_ROWS):
                first = ROW_FIRST + ROW_STEP * (a * BLOCKS + e)
                step = ROW_STEP * PLANE_ROWS
                nc.sync.dma_start(
                    v_planes[e:P:QUADRANT, a * S : (a + 1) * S].bitcast(I32),
                    picked_scales[first : first + step * (P // QUADRANT - 1) + 1 : step, :].bitcast(I32),
                )

        move_scales(0)
        load_table(1)
        move_scales(1)

        def quantise(grouped, width, name):
            codes = kept([P, width], U32, name + "_codes")
            plane = kept([P, width], U8, name + "_plane")
            nc.vector.quantize_mx(out=codes[:].bitcast(FP8X4), scales=plane[:], in_=grouped)
            return codes, plane

        down_mx = []
        for a in range(PASSES):
            grouped = kept([P, PACK * R], BF16, "down_grouped%d" % a, "slot_down_grouped%d" % a)
            nc.scalar.copy(
                grouped[:].rearrange("p (t m j) -> p m j t", t=PACK, j=PACK),
                down_raw[a][:].rearrange("p (j m t) -> p m j t", t=PACK, j=PACK),
            )
            down_mx.append(quantise(grouped[:], R, "down%d" % a))

        up_raw = kept([P, PACK * M], F32, "up_raw", "slot_up")
        nc.sync.dma_start(up_raw[:], up.rearrange("(p j) n -> p (j n)", j=PACK))
        bias_row = kept([P, M], F32, "bias_row", "h_grouped2")
        nc.vector.memset(bias_row[:], 0.0)
        nc.sync.dma_start(bias_row[BIAS_ROW : BIAS_ROW + 1, :], b.rearrange("(o n) -> o n", o=1))
        identity = kept([P, P], F32, "identity")
        make_identity(nc, identity[:])
        bias = kept([P, ROW_TILES], F32, "bias")
        for half in range(HALVES):
            bank = psum_y.tile([P, CHUNK], F32, name="y_bank")
            for u in range(HALF_TILES):
                columns = slice(half * CHUNK + u, (half + 1) * CHUNK, HALF_TILES)
                nc.tensor.transpose(bank[:, u * P : (u + 1) * P], bias_row[:, columns], identity[:])
            nc.scalar.copy(bias[:, half * HALF_TILES : (half + 1) * HALF_TILES], bank[:, BIAS_ROW:CHUNK:P])

        gates = []
        gate_slots = ["slot_w4_rows", "slot_table0", "slot_w4_raw", "slot_table1", "slot_up", "slot_up_grouped"]

        def load_gates():
            i = len(gates)
            g = kept([P, T], F32, "gates%d" % i, gate_slots[i % len(gate_slots)])
            nc.sync.dma_start(g[:], gT.rearrange("(u p i) t -> u i p t", u=HALVES, p=P)[i // HALF_TILES, i % HALF_TILES])
            gates.append(g)

        def list_slice(c):
            return offsets[:, c * LIST_COLS : (c + 1) * LIST_COLS]

        def deal(dealt, raw):
            nc.vector.tensor_copy(
                dealt.rearrange("p a (u i m) -> p a u m i", u=HALVES, i=HALF_TILES),
                raw.rearrange("p a (u m i) -> p a u m i", u=HALVES, i=HALF_TILES),
            )

        w4 = kept([P, PASSES, 2 * M], U8, "w4")
        w4_planes = kept([P, PASSES, M], U8, "w4_planes", "slot_down_grouped1")
        picked = {}
        for a in range(PASSES):
            for c in range(CHUNKS):
                picked[a, c] = kept([P, CHUNK], U32, "picked%d_%d" % (a, c))
                nc.vector.tensor_copy(picked[a, c][:], table[a][:].bitcast(U32).indirect(list_slice(c)))
            if a == 0:
                deal(w4_planes[:], w4_rows[:])
                deal(w4[:].bitcast(U16), w4_raw[:].bitcast(U16))
        while gate_slots[len(gates)] != "slot_up":
            load_gates()

        h_mx = []

        def make_h(c):
            grouped = kept([P, PACK * CHUNK], BF16, "h_grouped%d" % c)
            for s in range(CHUNK // P):
                bank = psum_h.tile([P, PACK, P], F32, name="h_bank")
                first = c * CHUNK + s * P
                for t in range(PACK):
                    for a in range(PASSES):
                        codes, plane = down_mx[a]
                        nc.tensor.matmul_mx(
                            out=bank[:, t, :],
                            lhsT=codes[:, t * P : (t + 1) * P].bitcast(FP8X4),
                            lhsT_scale=plane[:, t * P : (t + 1) * P],
                            rhs=picked[a, c][:, s * P : (s + 1) * P].bitcast(FP8X4),
                            rhs_scale=v_planes[:, a * S + first : a * S + first + P],
                            start=(a == 0),
                            stop=(a == PASSES - 1),
                        )
                nc.scalar.copy(
                    grouped[:, s * PACK * P : (s + 1) * PACK * P].rearrange("p (j t) -> p j t", t=PACK),
                    bank[:].rearrange("p t j -> p j t"),
                )
            h_mx.append(quantise(grouped[:], CHUNK, "h%d" % c))

        make_h(0)

        up_mx = []
        for half in range(HALVES):
            grouped = kept([P, PACK * HALF_TILES * P], BF16, "up_grouped%d" % half, "slot_up_grouped" if half else None)
            nc.vector.tensor_copy(
                grouped[:].rearrange("p (i m j) -> p m j i", i=HALF_TILES, j=PACK),
                up_raw[:].rearrange("p (j u m i) -> p u m j i", i=HALF_TILES, j=PACK, u=HALVES)[:, half],
            )
            up_mx.append(quantise(grouped[:], HALF_TILES * P, "up%d" % half))
        load_gates()
        load_gates()

        def gated_chunk(i, c, result):
            rows = slice(i * P, (i + 1) * P)
            bank = psum_y.tile([P, CHUNK], F32, name="y_bank")
            for a in range(PASSES):
                nc.tensor.matmul_mx(
                    out=bank[:],
                    lhsT=w4[:, a, 2 * i * P : 2 * (i + 1) * P].bitcast(FP4X4),
                    lhsT_scale=w4_planes[:, a, rows],
                    rhs=picked[a, c][:].bitcast(FP8X4),
                    rhs_scale=v_planes[:, a * S + c * CHUNK : a * S + (c + 1) * CHUNK],
                    start=(a == 0),
                    stop=False,
                )
            half, column = divmod(i * P, HALF_TILES * P)
            up_codes, up_plane = up_mx[half]
            h_codes, h_plane = h_mx[c]
            nc.tensor.matmul_mx(
                out=bank[:],
                lhsT=up_codes[:, column : column + P].bitcast(FP8X4),
                lhsT_scale=up_plane[:, column : column + P],
                rhs=h_codes[:].bitcast(FP8X4),
                rhs_scale=h_plane[:],
                start=False,
                stop=True,
            )
            act = acts.tile([P, CHUNK], F32, name="act")
            nc.scalar.activation(act[:], bank[:], gelu, bias=bias[:, i : i + 1])
            nc.vector.tensor_tensor(result, gates[i][:].indirect(list_slice(c)), act[:], mult)

        out_rows = out.rearrange("(u p i) s -> u p (i s)", u=HALVES, p=P)
        first_tile = 0
        for tiles in STORE_TILES:
            results = kept([P, tiles * S], F32, "results%d" % first_tile)
            for u in range(tiles):
                i = first_tile + u
                for c in range(CHUNKS):
                    if c == len(h_mx):
                        make_h(c)
                    gated_chunk(i, c, results[:, u * S + c * CHUNK : u * S + (c + 1) * CHUNK])
                if len(gates) < ROW_TILES:
                    load_gates()
            half, within = divmod(first_tile, HALF_TILES)
            nc.sync.dma_start(out_rows[half, :, within * S : (within + tiles) * S], results[:])
            first_tile = first_tile + tiles
